import numpy as np
import ml_dtypes


def mxq(x, axis, fmt="e4m3"):
    dtype, down = {"e4m3": (ml_dtypes.float8_e4m3fn, 7), "e5m2": (ml_dtypes.float8_e5m2, 14)}[fmt]
    v = np.moveaxis(np.asarray(x, np.float32).astype(ml_dtypes.bfloat16).astype(np.float64), axis, -1)
    blocks = v.reshape(v.shape[:-1] + (-1, 32))
    amax = np.abs(blocks).max(-1, keepdims=True)
    byte = np.maximum(np.where(amax > 0, np.frexp(amax)[1] - 1 + 127, 0) - down, 1)
    scale = np.exp2(byte - 127.0)
    codes = (blocks / scale).astype(np.float32).astype(dtype).astype(np.float64)
    return np.moveaxis((codes * scale).reshape(v.shape), -1, axis)


WIDE = False


def mx_kscale(k):
    if not WIDE:
        return np.ones(k)
    levels = np.array([10, -10, 5, -5, 0])
    if k % 512:
        return np.exp2(np.random.permutation(np.resize(levels, k // 32))).repeat(32)
    a = np.empty((k // 512, 16))
    for p in range(k // 512):
        a[p, :8] = np.random.permutation(np.resize(levels, 8))
        for g in range(8):
            far = levels[np.abs(levels - a[p, g]) >= 10]
            a[p, g + 8] = far[np.random.randint(len(far))]
    return np.exp2(a.ravel()).repeat(32)


def f64(x):
    return np.asarray(x).astype(np.float64)


def striped(idx):
    return np.tile(idx.reshape(-1, 16).T, (8, 1)).astype(np.uint16)


def unstriped(offs):
    return offs[:16].T.reshape(-1).astype(np.int64)


E2M1 = np.array([0.0, 0.5, 1.0, 1.5, 2.0, 3.0, 4.0, 6.0, -0.0, -0.5, -1.0, -1.5, -2.0, -3.0, -4.0, -6.0])


def pack_weight(w, fmt):
    k, n = w.shape
    w = f64(np.asarray(w, np.float32).astype(ml_dtypes.bfloat16)).reshape(k // 32, 32, n)
    amax = np.abs(w).max(1)
    if fmt == "e4m3":
        byte = np.frexp(amax)[1] - 1 + 127 - 7
    else:
        mant, ex = np.frexp(amax / 6.0)
        byte = np.where(mant > 0.5, ex, ex - 1) + 127
    byte = np.clip(np.where(amax > 0, byte, 1), 1, 254)
    scaled = (w * np.exp2(127.0 - byte)[:, None, :]).reshape(k, n).astype(np.float32)
    by_word = np.ascontiguousarray(scaled.reshape(k // 512, 128, 4, n).transpose(0, 1, 3, 2))
    if fmt == "e4m3":
        words = by_word.astype(ml_dtypes.float8_e4m3fn).view(np.uint8)
    else:
        c = by_word.astype(ml_dtypes.float4_e2m1fn).view(np.uint8) & 0xF
        words = (c[..., 0::2] | (c[..., 1::2] << 4)).reshape(k // 512, 128, 2 * n)
    return np.ascontiguousarray(words), np.ascontiguousarray(byte.astype(np.uint8).reshape(k // 512, 16, n))


def unpack_weight(words, scales, fmt):
    g, _, n = scales.shape
    words = np.ascontiguousarray(words).reshape(g, 128, n, -1)
    if fmt == "e4m3":
        vals = words.view(ml_dtypes.float8_e4m3fn).astype(np.float64)
    else:
        nib = np.empty((g, 128, n, 4), np.uint8)
        nib[..., 0::2] = words & 0xF
        nib[..., 1::2] = words >> 4
        vals = E2M1[nib]
    vals = vals * np.repeat(np.exp2(scales.astype(np.float64) - 127.0), 8, axis=1)[..., None]
    return vals.transpose(0, 1, 3, 2).reshape(g * 512, n)


def gelu(v):
    return 0.5 * v * (1.0 + np.tanh(np.sqrt(2.0 / np.pi) * (v + 0.044715 * v**3)))


K, K1, H, T, S, P = 1024, 512, 1024, 4096, 1024, 512

def setup_inputs():
    n = np.random.standard_normal
    s = mx_kscale(K)[:, None]
    u = mx_kscale(H)[:, None]
    tab_words, tab_scales = pack_weight(n((K, T)) * s, "e4m3")
    w4_words, w4_scales = pack_weight(1.5 * n((K - K1, H)) / np.sqrt(K) / s[K1:], "e2m1")
    return {
        "tab_words": tab_words,
        "tab_scales": tab_scales,
        "offs": striped(np.random.permutation(T)[:S]),
        "w1": (1.5 * n((K1, H)) / np.sqrt(K) / s[:K1]).astype(np.float32),
        "w4_words": w4_words,
        "w4_scales": w4_scales,
        "gain": (np.exp(0.3 * n(H)) * u[:, 0]).astype(np.float32),
        "law": (0.5 * n((H, S)) * u).astype(np.float32),
        "pos1": striped(np.random.permutation(S)[:P]),
        "pos2": striped(np.random.permutation(S)[:P]),
        "gv": (np.exp(0.3 * n(H)) / np.sqrt(H) / u[:, 0] ** 2).astype(np.float32),
        "rowv": np.exp(0.3 * n(P)).astype(np.float32),
        "colv": np.exp(0.3 * n(P)).astype(np.float32),
    }

def reference(tab_words, tab_scales, offs, w1, w4_words, w4_scales, gain, law, pos1, pos2, gv, rowv, colv):
    v = unpack_weight(tab_words, tab_scales, "e4m3")[:, unstriped(offs)]
    w4 = unpack_weight(w4_words, w4_scales, "e2m1")
    w1q = mxq(f64(w1), 0, "e4m3")
    y = w1q.T @ v[:K1] + w4.T @ v[K1:]
    h = np.tanh(y) * f64(gain)[:, None] + f64(law)
    x1 = h[:, unstriped(pos1)]
    x2 = np.abs(h[:, unstriped(pos2)]) * f64(gv)[:, None]
    e = mxq(x1, 0, "e4m3").T @ mxq(x2, 0, "e4m3")
    return e * f64(rowv)[None, :] * f64(colv)[:, None]

@@ -1,0 +1,246 @@
+from contextlib import ExitStack
+
+import concourse.mybir as mybir
+
+F32 = mybir.dt.float32
+BF16 = mybir.dt.bfloat16
+I32 = mybir.dt.int32
+U32 = mybir.dt.uint32
+U16 = mybir.dt.uint16
+U8 = mybir.dt.uint8
+FP8X4 = mybir.dt.float8_e4m3fn_x4
+FP4X4 = mybir.dt.float4_e2m1fn_x4
+MULT = mybir.AluOpType.mult
+ADD = mybir.AluOpType.add
+ACT = mybir.ActivationFunctionType
+
+P = 128
+PACK = 4
+KP = P * PACK
+H, T, S, M = 1024, 4096, 1024, 512
+NB = H // KP
+BANK = 512
+
+FLOPS = 2 * 1024 * H * S + 2 * H * M * M
+
+
+def tile_list_cognate_candidate_scores_kernel(
+    tc, tab_words, tab_scales, offs, w1, w4_words, w4_scales, gain, law, pos1, pos2, gv, rowv, colv, out
+):
+    nc = tc.nc
+    with ExitStack() as ctx:
+        keep = ctx.enter_context(tc.tile_pool(name="keep", bufs=1))
+        ring = ctx.enter_context(tc.tile_pool(name="ring", bufs=2))
+        psum = ctx.enter_context(tc.psum_pool(name="psum", bufs=1))
+
+        offs_t = keep.tile([P, S // 16], U16, name="offs_t")
+        pos1_t = keep.tile([P, M // 16], U16, name="pos1_t")
+        pos2_t = keep.tile([P, M // 16], U16, name="pos2_t")
+        tabw = [keep.tile([P, T], U32, name=f"tabw{a}", align_bytes=64) for a in range(2)]
+        tabs = keep.tile([P, T], U8, name="tabs", align_bytes=64)
+        w4s_raw = keep.tile([P, H], U8, name="w4s_raw", align_bytes=64)
+        w4w_raw = keep.tile([P, 2 * H], U8, name="w4w_raw", align_bytes=64)
+        w1_raw = [keep.tile([P, PACK, KP], F32, name=f"w1_raw{b}", align_bytes=64) for b in range(NB)]
+        law_t = [keep.tile([P, S], F32, name=f"law{i}", align_bytes=64) for i in range(NB * PACK)]
+        gain_t = keep.tile([P, NB, PACK], F32, name="gain_t")
+        gv_t = keep.tile([P, NB, PACK], F32, name="gv_t")
+        colv_t = keep.tile([P, M // P], F32, name="colv_t")
+        rowv_t = keep.tile([P, M], F32, name="rowv_t")
+
+        nc.vector.memset(w4s_raw[:].bitcast(I32), 0)
+        nc.vector.memset(tabs[:, : T // 2].bitcast(I32), 0)
+        nc.gpsimd.memset(tabs[:, T // 2 :].bitcast(I32), 0)
+
+        def load_law(i):
+            b, t = divmod(i, PACK)
+            rows = law[b * KP : (b + 1) * KP, :].rearrange("(p t) n -> p t n", t=PACK)
+            nc.sync.dma_start(out=law_t[i][:], in_=rows[:, t, :])
+
+        def load_w1(b):
+            nc.sync.dma_start(
+                out=w1_raw[b][:], in_=w1.rearrange("(p j) c -> p j c", j=PACK)[:, :, b * KP : (b + 1) * KP]
+            )
+
+        def load_tab(a):
+            nc.sync.dma_start(
+                out=tabw[a][:].bitcast(I32), in_=tab_words[a].rearrange("p t i -> p (t i)").bitcast(I32)
+            )
+
+        nc.sync.dma_start(offs_t[:], offs)
+        nc.sync.dma_start(pos2_t[:], pos2)
+        nc.sync.dma_start(out=w4w_raw[:].bitcast(I32), in_=w4_words[0].bitcast(I32))
+        for q in range(4):
+            nc.sync.dma_start(
+                out=w4s_raw[32 * q : 32 * q + 4, :].bitcast(I32), in_=w4_scales[0, 4 * q : 4 * q + 4, :].bitcast(I32)
+            )
+        load_w1(0)
+        for n in range(8):
+            if n == 2:
+                load_tab(0)
+            a, q = n % 2, (n // 2) % 2 * 2 + n // 4
+            first = 32 * q + 4 * (1 - a)
+            nc.sync.dma_start(
+                out=tabs[first : first + 4, :].bitcast(I32), in_=tab_scales[a, 4 * q : 4 * q + 4, :].bitcast(I32)
+            )
+        load_tab(1)
+        load_law(0)
+        nc.sync.dma_start(out=gain_t[:], in_=gain.rearrange("(b p t) -> p b t", p=P, t=PACK))
+        nc.sync.dma_start(pos1_t[:], pos1)
+        load_w1(1)
+        load_law(1)
+        nc.sync.dma_start(out=gv_t[:], in_=gv.rearrange("(b p t) -> p b t", p=P, t=PACK))
+        for i in range(2, NB * PACK):
+            load_law(i)
+        with nc.allow_non_contiguous_dma(reason="one factor a partition"):
+            nc.sync.dma_start(out=colv_t[:], in_=colv.rearrange("(c p) -> p c", p=P))
+        nc.sync.dma_start(out=rowv_t[:], in_=rowv.partition_broadcast(P))
+
+        w1_codes = keep.tile([P, H], U32, name="w1_codes", align_bytes=64)
+        w1_scales = keep.tile([P, H], U8, name="w1_scales", align_bytes=64)
+
+        def prepare_w1(b):
+            grouped = ring.tile([P, KP * PACK], BF16, name="w1_grouped", align_bytes=64, bufs=1)
+            nc.scalar.copy(
+                out=grouped[:].rearrange("p (t m j) -> p m j t", t=PACK, j=PACK),
+                in_=w1_raw[b][:].rearrange("p j (m t) -> p m j t", t=PACK),
+            )
+            cols = slice(b * KP, (b + 1) * KP)
+            nc.vector.quantize_mx(out=w1_codes[:, cols].bitcast(FP8X4), scales=w1_scales[:, cols], in_=grouped[:])
+
+        vw = [keep.tile([P, S], U32, name=f"vw{a}", align_bytes=64) for a in range(2)]
+        vs = keep.tile([P, S], U8, name="vs", align_bytes=64)
+        w4w = keep.tile([P, 2 * H], U8, name="w4w", align_bytes=64)
+        w4s = keep.tile([P, H], U8, name="w4s", align_bytes=64)
+
+        nc.vector.tensor_copy(
+            out=w4w[:].bitcast(U16).rearrange("p (b t m) -> p b t m", b=NB, t=PACK),
+            in_=w4w_raw[:].bitcast(U16).rearrange("p (b m t) -> p b t m", b=NB, t=PACK),
+        )
+        nc.vector.tensor_copy(
+            out=w4s[:].rearrange("p (b t m) -> p b t m", b=NB, t=PACK),
+            in_=w4s_raw[:].rearrange("p (b m t) -> p b t m", b=NB, t=PACK),
+        )
+        prepare_w1(0)
+        nc.vector.tensor_copy(vw[0][:], tabw[0][:].indirect(offs_t[:]))
+        nc.vector.tensor_copy(vs[:], tabs[:].indirect(offs_t[:]))
+        bank_cuts = [slice(u * BANK, (u + 1) * BANK) for u in range(S // BANK)]
+        for cols in bank_cuts:
+            nc.vector.tensor_copy(vw[1][:, cols], tabw[1][:].indirect(offs_t[:, cols.start // 16 : cols.stop // 16]))
+
+        th = {}
+        banks = [f"bank{n}" for n in range(8)]
+
+        def w1_pass(i, cols, bank):
+            y = psum.tile([P, BANK], F32, name="y", tag=bank)
+            ch = slice(i * P, (i + 1) * P)
+            nc.tensor.matmul_mx(
+                out=y[:, : cols.stop - cols.start],
+                lhsT=w1_codes[:, ch].bitcast(FP8X4),
+                lhsT_scale=w1_scales[:, ch],
+                rhs=vw[0][:, cols].bitcast(FP8X4),
+                rhs_scale=vs[4:P, cols],
+                start=True,
+                stop=False,
+            )
+            return y
+
+        def w4_pass(i, cols, y):
+            nc.tensor.matmul_mx(
+                out=y[:, : cols.stop - cols.start],
+                lhsT=w4w[:, 2 * i * P : 2 * (i + 1) * P].bitcast(FP4X4),
+                lhsT_scale=w4s[:, i * P : (i + 1) * P],
+                rhs=vw[1][:, cols].bitcast(FP8X4),
+                rhs_scale=vs[:, cols],
+                start=False,
+                stop=True,
+            )
+            nc.scalar.activation(out=th[i][:, cols], in_=y[:, : cols.stop - cols.start], func=ACT.Tanh)
+
+        def first_stage(i):
+            th[i] = keep.tile([P, S], F32, name=f"th{i}", align_bytes=64)
+            for u, cols in enumerate(bank_cuts):
+                w4_pass(i, cols, w1_pass(i, cols, banks[(2 * i + u) % 4]))
+
+        x2r = [keep.tile([P, PACK, M], BF16, name=f"x2r{b}", align_bytes=64) for b in range(NB)]
+        n_tiles = NB * PACK
+
+        def features(i):
+            b, t = divmod(i, PACK)
+            for cols in bank_cuts if i == 0 else [slice(0, S)]:
+                nc.vector.scalar_tensor_tensor(
+                    out=th[i][:, cols],
+                    in0=th[i][:, cols],
+                    scalar=gain_t[:, b, t : t + 1],
+                    in1=law_t[i][:, cols],
+                    op0=MULT,
+                    op1=ADD,
+                )
+
+        def pick2(i):
+            b, t = divmod(i, PACK)
+            g2 = keep.tile([P, M], F32, name=f"g2_{i}")
+            nc.vector.tensor_copy(g2[:], th[i][:].indirect(pos2_t[:]))
+            a2 = ring.tile([P, M], F32, name="a2", bufs=2)
+            nc.scalar.activation(out=a2[:], in_=g2[:], func=ACT.Abs)
+            nc.scalar.activation(out=x2r[b][:, t, :], in_=a2[:], func=ACT.Copy, scale=gv_t[:, b, t : t + 1])
+
+        def pick1(i):
+            nc.vector.tensor_copy(x1r[:, i, :], th[i][:].indirect(pos1_t[:]))
+
+
+        def weave_and_quantise(src, cols, name):
+            width = cols.stop - cols.start
+            woven = keep.tile([P, width * PACK], BF16, name=name + "_woven", align_bytes=64)
+            nc.scalar.copy(
+                out=woven[:].rearrange("p (c i t) -> p c t i", i=4, t=PACK),
+                in_=src[:, :, cols].rearrange("p t (c i) -> p c t i", i=4),
+            )
+            codes = keep.tile([P, width], U32, name=name + "_codes", align_bytes=64)
+            scales = keep.tile([P, width], U8, name=name + "_scales", align_bytes=64)
+            nc.vector.quantize_mx(out=codes[:].bitcast(FP8X4), scales=scales[:], in_=woven[:])
+            return codes, scales
+
+        def score(c, b, c1, s1, c2, s2):
+            nc.tensor.matmul_mx(
+                out=e[c][:],
+                lhsT=c1.bitcast(FP8X4),
+                lhsT_scale=s1,
+                rhs=c2[:].bitcast(FP8X4),
+                rhs_scale=s2[:],
+                start=(b == 0),
+                stop=(b == NB - 1),
+            )
+
+        th[0] = keep.tile([P, S], F32, name="th0", align_bytes=64)
+        opened = [w1_pass(0, cols, banks[u]) for u, cols in enumerate(bank_cuts)]
+        for cols, y in zip(bank_cuts, opened):
+            w4_pass(0, cols, y)
+        first_stage(1)
+        prepare_w1(1)
+        for i in range(2, n_tiles):
+            first_stage(i)
+        e = [psum.tile([P, M], F32, name="e", tag=banks[4 + c]) for c in range(M // P)]
+        x2q = {}
+        features(0)
+        for i in range(n_tiles):
+            if i + 1 < n_tiles:
+                features(i + 1)
+            pick2(i)
+            if i % PACK == PACK - 1:
+                x2q[i // PACK] = weave_and_quantise(x2r[i // PACK][:], slice(0, M), f"x2_{i // PACK}")
+        x1r = keep.tile([P, n_tiles, M], BF16, name="x1r", tag=f"law{n_tiles - 1}", align_bytes=64)
+        for i in range(n_tiles):
+            pick1(i)
+        c1, s1 = weave_and_quantise(x1r[:, :PACK, :], slice(0, M), "x1_0")
+        for c in range(M // P):
+            score(c, 0, c1[:, c * P : (c + 1) * P], s1[:, c * P : (c + 1) * P], *x2q[0])
+        for c in range(M // P):
+            c1, s1 = weave_and_quantise(x1r[:, PACK:, :], slice(c * P, (c + 1) * P), f"x1_1_{c}")
+            score(c, 1, c1[:], s1[:], *x2q[1])
+
+        for c in range(M // P):
+            res = ring.tile([P, M], F32, name="res", bufs=4)
+            nc.vector.scalar_tensor_tensor(
+                out=res[:], in0=e[c][:], scalar=colv_t[:, c : c + 1], in1=rowv_t[:], op0=MULT, op1=MULT
+            )
+            nc.sync.dma_start(out=out[c * P : (c + 1) * P, :], in_=res[:])

@@ -70,24 +70,20 @@ def tile_list_cognate_candidate_scores_kernel(
         nc.sync.dma_start(pos2_t[:], pos2)
         nc.sync.dma_start(out=w4w_raw[:].bitcast(I32), in_=w4_words[0].bitcast(I32))
         for q in range(4):
-            nc.sync.dma_start(
-                out=w4s_raw[32 * q : 32 * q + 4, :].bitcast(I32), in_=w4_scales[0, 4 * q : 4 * q + 4, :].bitcast(I32)
-            )
+            nc.sync.dma_start(out=w4s_raw[q:P:32, :].bitcast(I32), in_=w4_scales[0, q:16:4, :].bitcast(I32))
         load_w1(0)
         for n in range(8):
             if n == 2:
                 load_tab(0)
-            a, q = n % 2, (n // 2) % 2 * 2 + n // 4
-            first = 32 * q + 4 * (1 - a)
-            nc.sync.dma_start(
-                out=tabs[first : first + 4, :].bitcast(I32), in_=tab_scales[a, 4 * q : 4 * q + 4, :].bitcast(I32)
-            )
+            r, a = divmod(n, 2)
+            first = 4 * (1 - a) + r
+            nc.sync.dma_start(out=tabs[first:P:32, :].bitcast(I32), in_=tab_scales[a, r:16:4, :].bitcast(I32))
         load_tab(1)
+        load_w1(1)
         load_law(0)
         nc.sync.dma_start(out=gain_t[:], in_=gain.rearrange("(b p t) -> p b t", p=P, t=PACK))
-        nc.sync.dma_start(pos1_t[:], pos1)
-        load_w1(1)
         load_law(1)
+        nc.sync.dma_start(pos1_t[:], pos1)
         nc.sync.dma_start(out=gv_t[:], in_=gv.rearrange("(b p t) -> p b t", p=P, t=PACK))
         for i in range(2, NB * PACK):
             load_law(i)
@@ -100,10 +96,11 @@ def tile_list_cognate_candidate_scores_kernel(
 
         def prepare_w1(b):
             grouped = ring.tile([P, KP * PACK], BF16, name="w1_grouped", align_bytes=64, bufs=1)
-            nc.scalar.copy(
-                out=grouped[:].rearrange("p (t m j) -> p m j t", t=PACK, j=PACK),
-                in_=w1_raw[b][:].rearrange("p j (m t) -> p m j t", t=PACK),
-            )
+            for m0 in range(0, P, P // 4):
+                nc.scalar.copy(
+                    out=grouped[:].rearrange("p (t m j) -> p m j t", t=PACK, j=PACK)[:, m0 : m0 + P // 4],
+                    in_=w1_raw[b][:].rearrange("p j (m t) -> p m j t", t=PACK)[:, m0 : m0 + P // 4],
+                )
             cols = slice(b * KP, (b + 1) * KP)
             nc.vector.quantize_mx(out=w1_codes[:, cols].bitcast(FP8X4), scales=w1_scales[:, cols], in_=grouped[:])
 
@@ -185,19 +182,18 @@ def tile_list_cognate_candidate_scores_kernel(
             nc.scalar.activation(out=x2r[b][:, t, :], in_=a2[:], func=ACT.Copy, scale=gv_t[:, b, t : t + 1])
 
         def pick1(i):
-            nc.vector.tensor_copy(x1r[:, i, :], th[i][:].indirect(pos1_t[:]))
+            nc.vector.tensor_copy(x1r[i // PACK][:, i % PACK, :], th[i][:].indirect(pos1_t[:]))
 
 
-        def weave_and_quantise(src, cols, name):
+        def weave_and_quantise(src, cols, woven, name):
             width = cols.stop - cols.start
-            woven = keep.tile([P, width * PACK], BF16, name=name + "_woven", align_bytes=64)
             nc.scalar.copy(
-                out=woven[:].rearrange("p (c i t) -> p c t i", i=4, t=PACK),
+                out=woven.rearrange("p (c i t) -> p c t i", i=4, t=PACK),
                 in_=src[:, :, cols].rearrange("p t (c i) -> p c t i", i=4),
             )
             codes = keep.tile([P, width], U32, name=name + "_codes", align_bytes=64)
             scales = keep.tile([P, width], U8, name=name + "_scales", align_bytes=64)
-            nc.vector.quantize_mx(out=codes[:].bitcast(FP8X4), scales=scales[:], in_=woven[:])
+            nc.vector.quantize_mx(out=codes[:].bitcast(FP8X4), scales=scales[:], in_=woven)
             return codes, scales
 
         def score(c, b, c1, s1, c2, s2):
@@ -227,20 +223,29 @@ def tile_list_cognate_candidate_scores_kernel(
                 features(i + 1)
             pick2(i)
             if i % PACK == PACK - 1:
-                x2q[i // PACK] = weave_and_quantise(x2r[i // PACK][:], slice(0, M), f"x2_{i // PACK}")
-        x1r = keep.tile([P, n_tiles, M], BF16, name="x1r", tag=f"law{n_tiles - 1}", align_bytes=64)
-        for i in range(n_tiles):
-            pick1(i)
-        c1, s1 = weave_and_quantise(x1r[:, :PACK, :], slice(0, M), "x1_0")
+                woven = keep.tile([P, M * PACK], BF16, name=f"x2_woven{i // PACK}", align_bytes=64)
+                x2q[i // PACK] = weave_and_quantise(x2r[i // PACK][:], slice(0, M), woven[:], f"x2_{i // PACK}")
+        x1r = {}
+        for b, tag in enumerate([f"law{n_tiles - 1}", "th0"]):
+            x1r[b] = keep.tile([P, PACK, M], BF16, name="x1r", tag=tag, align_bytes=64)
+            for t in range(PACK):
+                pick1(b * PACK + t)
+        woven = keep.tile([P, M * PACK], BF16, name="x1_woven0", tag=f"x2r{NB - 1}", align_bytes=64)
+        c1, s1 = weave_and_quantise(x1r[0][:], slice(0, M), woven[:], "x1_0")
         for c in range(M // P):
             score(c, 0, c1[:, c * P : (c + 1) * P], s1[:, c * P : (c + 1) * P], *x2q[0])
-        for c in range(M // P):
-            c1, s1 = weave_and_quantise(x1r[:, PACK:, :], slice(c * P, (c + 1) * P), f"x1_1_{c}")
-            score(c, 1, c1[:], s1[:], *x2q[1])
-
-        for c in range(M // P):
-            res = ring.tile([P, M], F32, name="res", bufs=4)
-            nc.vector.scalar_tensor_tensor(
-                out=res[:], in0=e[c][:], scalar=colv_t[:, c : c + 1], in1=rowv_t[:], op0=MULT, op1=MULT
+        woven = keep.tile([P, M * PACK], BF16, name="x1_woven1", tag=f"law{n_tiles - 1}", align_bytes=64)
+        for half in range(2):
+            cols = slice(half * M // 2, (half + 1) * M // 2)
+            c1, s1 = weave_and_quantise(
+                x1r[1][:], cols, woven[:, cols.start * PACK : cols.stop * PACK], f"x1_1_{half}"
             )
-            nc.sync.dma_start(out=out[c * P : (c + 1) * P, :], in_=res[:])
+            for c in range(2):
+                score(2 * half + c, 1, c1[:, c * P : (c + 1) * P], s1[:, c * P : (c + 1) * P], *x2q[1])
+
+        res = keep.tile([P, M // P, M], F32, name="res", tag=f"law{n_tiles - 1}", align_bytes=64)
+        for c in range(M // P):
+            nc.vector.scalar_tensor_tensor(
+                out=res[:, c, :], in0=e[c][:], scalar=colv_t[:, c : c + 1], in1=rowv_t[:], op0=MULT, op1=MULT
+            )
+            nc.sync.dma_start(out=out[c * P : (c + 1) * P, :], in_=res[:, c, :])

@@ -69,9 +69,9 @@ def tile_list_cognate_candidate_scores_kernel(
         nc.sync.dma_start(offs_t[:], offs)
         nc.sync.dma_start(pos2_t[:], pos2)
         nc.sync.dma_start(out=w4w_raw[:].bitcast(I32), in_=w4_words[0].bitcast(I32))
+        load_w1(0)
         for q in range(4):
             nc.sync.dma_start(out=w4s_raw[q:P:32, :].bitcast(I32), in_=w4_scales[0, q:16:4, :].bitcast(I32))
-        load_w1(0)
         for n in range(8):
             if n == 2:
                 load_tab(0)
@@ -79,9 +79,9 @@ def tile_list_cognate_candidate_scores_kernel(
             first = 4 * (1 - a) + r
             nc.sync.dma_start(out=tabs[first:P:32, :].bitcast(I32), in_=tab_scales[a, r:16:4, :].bitcast(I32))
         load_tab(1)
-        load_w1(1)
         load_law(0)
         nc.sync.dma_start(out=gain_t[:], in_=gain.rearrange("(b p t) -> p b t", p=P, t=PACK))
+        load_w1(1)
         load_law(1)
         nc.sync.dma_start(pos1_t[:], pos1)
         nc.sync.dma_start(out=gv_t[:], in_=gv.rearrange("(b p t) -> p b t", p=P, t=PACK))
@@ -98,8 +98,8 @@ def tile_list_cognate_candidate_scores_kernel(
             grouped = ring.tile([P, KP * PACK], BF16, name="w1_grouped", align_bytes=64, bufs=1)
             for m0 in range(0, P, P // 4):
                 nc.scalar.copy(
-                    out=grouped[:].rearrange("p (t m j) -> p m j t", t=PACK, j=PACK)[:, m0 : m0 + P // 4],
-                    in_=w1_raw[b][:].rearrange("p j (m t) -> p m j t", t=PACK)[:, m0 : m0 + P // 4],
+                    out=grouped[:].rearrange("p (t m j) -> p m t j", t=PACK, j=PACK)[:, m0 : m0 + P // 4],
+                    in_=w1_raw[b][:].rearrange("p j (m t) -> p m t j", t=PACK)[:, m0 : m0 + P // 4],
                 )
             cols = slice(b * KP, (b + 1) * KP)
             nc.vector.quantize_mx(out=w1_codes[:, cols].bitcast(FP8X4), scales=w1_scales[:, cols], in_=grouped[:])
@@ -161,25 +161,30 @@ def tile_list_cognate_candidate_scores_kernel(
         x2r = [keep.tile([P, PACK, M], BF16, name=f"x2r{b}", align_bytes=64) for b in range(NB)]
         n_tiles = NB * PACK
 
-        def features(i):
+        def features(i, cols):
             b, t = divmod(i, PACK)
-            for cols in bank_cuts if i == 0 else [slice(0, S)]:
-                nc.vector.scalar_tensor_tensor(
-                    out=th[i][:, cols],
-                    in0=th[i][:, cols],
-                    scalar=gain_t[:, b, t : t + 1],
-                    in1=law_t[i][:, cols],
-                    op0=MULT,
-                    op1=ADD,
-                )
+            nc.vector.scalar_tensor_tensor(
+                out=th[i][:, cols],
+                in0=th[i][:, cols],
+                scalar=gain_t[:, b, t : t + 1],
+                in1=law_t[i][:, cols],
+                op0=MULT,
+                op1=ADD,
+            )
 
-        def pick2(i):
+        def features_on_gpsimd(i, scaled):
+            b, t = divmod(i, PACK)
+            nc.gpsimd.tensor_scalar(
+                out=scaled, in0=th[i][:], scalar1=gain_t[:, b, t : t + 1], scalar2=0.0, op0=MULT, op1=ADD
+            )
+            nc.gpsimd.tensor_tensor(out=th[i][:], in0=scaled, in1=law_t[i][:], op=ADD)
+
+        def pick2(i, a2):
             b, t = divmod(i, PACK)
             g2 = keep.tile([P, M], F32, name=f"g2_{i}")
             nc.vector.tensor_copy(g2[:], th[i][:].indirect(pos2_t[:]))
-            a2 = ring.tile([P, M], F32, name="a2", bufs=2)
-            nc.scalar.activation(out=a2[:], in_=g2[:], func=ACT.Abs)
-            nc.scalar.activation(out=x2r[b][:, t, :], in_=a2[:], func=ACT.Copy, scale=gv_t[:, b, t : t + 1])
+            nc.scalar.activation(out=a2, in_=g2[:], func=ACT.Abs)
+            nc.scalar.activation(out=x2r[b][:, t, :], in_=a2, func=ACT.Copy, scale=gv_t[:, b, t : t + 1])
 
         def pick1(i):
             nc.vector.tensor_copy(x1r[i // PACK][:, i % PACK, :], th[i][:].indirect(pos1_t[:]))
@@ -217,33 +222,50 @@ def tile_list_cognate_candidate_scores_kernel(
             first_stage(i)
         e = [psum.tile([P, M], F32, name="e", tag=banks[4 + c]) for c in range(M // P)]
         x2q = {}
-        features(0)
-        for i in range(n_tiles):
-            if i + 1 < n_tiles:
-                features(i + 1)
-            pick2(i)
-            if i % PACK == PACK - 1:
-                woven = keep.tile([P, M * PACK], BF16, name=f"x2_woven{i // PACK}", align_bytes=64)
-                x2q[i // PACK] = weave_and_quantise(x2r[i // PACK][:], slice(0, M), woven[:], f"x2_{i // PACK}")
         x1r = {}
-        for b, tag in enumerate([f"law{n_tiles - 1}", "th0"]):
-            x1r[b] = keep.tile([P, PACK, M], BF16, name="x1r", tag=tag, align_bytes=64)
-            for t in range(PACK):
-                pick1(b * PACK + t)
-        woven = keep.tile([P, M * PACK], BF16, name="x1_woven0", tag=f"x2r{NB - 1}", align_bytes=64)
-        c1, s1 = weave_and_quantise(x1r[0][:], slice(0, M), woven[:], "x1_0")
+
+        def finish_x2(b):
+            woven = keep.tile([P, M * PACK], BF16, name=f"x2_woven{b}", align_bytes=64)
+            x2q[b] = weave_and_quantise(x2r[b][:], slice(0, M), woven[:], f"x2_{b}")
+
+        for cols in bank_cuts:
+            features(0, cols)
+        early = n_tiles - 2
+        for i in range(early):
+            if i + 1 < early:
+                features(i + 1, slice(0, S))
+            a2 = keep.tile([P, M], F32, name=f"a2_{i % 2}", align_bytes=64)
+            pick2(i, a2[:])
+            if i == PACK - 1:
+                finish_x2(0)
+        first = keep.tile([P, PACK * M + S], F32, name="first", tag=f"law{early - 1}", align_bytes=64)
+        x1r[0] = first[:, : PACK * M].rearrange("p (t m) -> p t m", t=PACK)
+        for i in range(early, n_tiles):
+            features_on_gpsimd(i, first[:, PACK * M :])
+        for t in range(PACK):
+            pick1(t)
+        shared = keep.tile([P, (PACK + 2) * M], F32, name="shared", tag=f"a2_{(early - 1) % 2}", align_bytes=64)
+        c1, s1 = weave_and_quantise(
+            x1r[0], slice(0, M), shared[:, (PACK - 1) * M : (PACK + 1) * M].bitcast(BF16), "x1_0"
+        )
+        for i in range(early, n_tiles):
+            pick2(i, shared[:, (PACK + 1) * M :])
         for c in range(M // P):
             score(c, 0, c1[:, c * P : (c + 1) * P], s1[:, c * P : (c + 1) * P], *x2q[0])
-        woven = keep.tile([P, M * PACK], BF16, name="x1_woven1", tag=f"law{n_tiles - 1}", align_bytes=64)
+        x1r[1] = shared[:, : PACK * M].rearrange("p (t m) -> p t m", t=PACK)
+        for t in range(PACK):
+            pick1(PACK + t)
+        finish_x2(1)
+        woven = keep.tile([P, M * PACK], BF16, name="x1_woven1", tag=f"x2r{NB - 1}", align_bytes=64)
         for half in range(2):
             cols = slice(half * M // 2, (half + 1) * M // 2)
             c1, s1 = weave_and_quantise(
-                x1r[1][:], cols, woven[:, cols.start * PACK : cols.stop * PACK], f"x1_1_{half}"
+                x1r[1], cols, woven[:, cols.start * PACK : cols.stop * PACK], f"x1_1_{half}"
             )
             for c in range(2):
                 score(2 * half + c, 1, c1[:, c * P : (c + 1) * P], s1[:, c * P : (c + 1) * P], *x2q[1])
 
-        res = keep.tile([P, M // P, M], F32, name="res", tag=f"law{n_tiles - 1}", align_bytes=64)
+        res = keep.tile([P, M // P, M], F32, name="res", tag=f"x2r{NB - 1}", align_bytes=64)
         for c in range(M // P):
             nc.vector.scalar_tensor_tensor(
                 out=res[:, c, :], in0=e[c][:], scalar=colv_t[:, c : c + 1], in1=rowv_t[:], op0=MULT, op1=MULT

from contextlib import ExitStack

import concourse.mybir as mybir

F32 = mybir.dt.float32
BF16 = mybir.dt.bfloat16
I32 = mybir.dt.int32
U32 = mybir.dt.uint32
U16 = mybir.dt.uint16
U8 = mybir.dt.uint8
FP8X4 = mybir.dt.float8_e4m3fn_x4
FP4X4 = mybir.dt.float4_e2m1fn_x4
MULT = mybir.AluOpType.mult
ADD = mybir.AluOpType.add
ACT = mybir.ActivationFunctionType

P = 128
PACK = 4
KP = P * PACK
H, T, S, M = 1024, 4096, 1024, 512
NB = H // KP
BANK = 512

FLOPS = 2 * 1024 * H * S + 2 * H * M * M


def tile_list_cognate_candidate_scores_kernel(
    tc, tab_words, tab_scales, offs, w1, w4_words, w4_scales, gain, law, pos1, pos2, gv, rowv, colv, out
):
    nc = tc.nc
    with ExitStack() as ctx:
        keep = ctx.enter_context(tc.tile_pool(name="keep", bufs=1))
        ring = ctx.enter_context(tc.tile_pool(name="ring", bufs=2))
        psum = ctx.enter_context(tc.psum_pool(name="psum", bufs=1))

        offs_t = keep.tile([P, S // 16], U16, name="offs_t")
        pos1_t = keep.tile([P, M // 16], U16, name="pos1_t")
        pos2_t = keep.tile([P, M // 16], U16, name="pos2_t")
        tabw = [keep.tile([P, T], U32, name=f"tabw{a}", align_bytes=64) for a in range(2)]
        tabs = keep.tile([P, T], U8, name="tabs", align_bytes=64)
        w4s_raw = keep.tile([P, H], U8, name="w4s_raw", align_bytes=64)
        w4w_raw = keep.tile([P, 2 * H], U8, name="w4w_raw", align_bytes=64)
        w1_raw = [keep.tile([P, PACK, KP], F32, name=f"w1_raw{b}", align_bytes=64) for b in range(NB)]
        law_t = [keep.tile([P, S], F32, name=f"law{i}", align_bytes=64) for i in range(NB * PACK)]
        gain_t = keep.tile([P, NB, PACK], F32, name="gain_t")
        gv_t = keep.tile([P, NB, PACK], F32, name="gv_t")
        colv_t = keep.tile([P, M // P], F32, name="colv_t")
        rowv_t = keep.tile([P, M], F32, name="rowv_t")

        nc.vector.memset(w4s_raw[:].bitcast(I32), 0)
        nc.vector.memset(tabs[:, : T // 2].bitcast(I32), 0)
        nc.gpsimd.memset(tabs[:, T // 2 :].bitcast(I32), 0)

        def load_law(i):
            b, t = divmod(i, PACK)
            rows = law[b * KP : (b + 1) * KP, :].rearrange("(p t) n -> p t n", t=PACK)
            nc.sync.dma_start(out=law_t[i][:], in_=rows[:, t, :])

        def load_w1(b):
            nc.sync.dma_start(
                out=w1_raw[b][:], in_=w1.rearrange("(p j) c -> p j c", j=PACK)[:, :, b * KP : (b + 1) * KP]
            )

        def load_tab(a):
            nc.sync.dma_start(
                out=tabw[a][:].bitcast(I32), in_=tab_words[a].rearrange("p t i -> p (t i)").bitcast(I32)
            )

        nc.sync.dma_start(offs_t[:], offs)
        nc.sync.dma_start(pos2_t[:], pos2)
        nc.sync.dma_start(out=w4w_raw[:].bitcast(I32), in_=w4_words[0].bitcast(I32))
        load_w1(0)
        for q in range(4):
            nc.sync.dma_start(out=w4s_raw[q:P:32, :].bitcast(I32), in_=w4_scales[0, q:16:4, :].bitcast(I32))
        for n in range(8):
            if n == 2:
                load_tab(0)
            r, a = divmod(n, 2)
            first = 4 * (1 - a) + r
            nc.sync.dma_start(out=tabs[first:P:32, :].bitcast(I32), in_=tab_scales[a, r:16:4, :].bitcast(I32))
        load_tab(1)
        load_law(0)
        nc.sync.dma_start(out=gain_t[:], in_=gain.rearrange("(b p t) -> p b t", p=P, t=PACK))
        load_w1(1)
        load_law(1)
        nc.sync.dma_start(pos1_t[:], pos1)
        nc.sync.dma_start(out=gv_t[:], in_=gv.rearrange("(b p t) -> p b t", p=P, t=PACK))
        for i in range(2, NB * PACK):
            load_law(i)
        with nc.allow_non_contiguous_dma(reason="one factor a partition"):
            nc.sync.dma_start(out=colv_t[:], in_=colv.rearrange("(c p) -> p c", p=P))
        nc.sync.dma_start(out=rowv_t[:], in_=rowv.partition_broadcast(P))

        w1_codes = keep.tile([P, H], U32, name="w1_codes", align_bytes=64)
        w1_scales = keep.tile([P, H], U8, name="w1_scales", align_bytes=64)

        def prepare_w1(b):
            grouped = ring.tile([P, KP * PACK], BF16, name="w1_grouped", align_bytes=64, bufs=1)
            for m0 in range(0, P, P // 4):
                nc.scalar.copy(
                    out=grouped[:].rearrange("p (t m j) -> p m t j", t=PACK, j=PACK)[:, m0 : m0 + P // 4],
                    in_=w1_raw[b][:].rearrange("p j (m t) -> p m t j", t=PACK)[:, m0 : m0 + P // 4],
                )
            cols = slice(b * KP, (b + 1) * KP)
            nc.vector.quantize_mx(out=w1_codes[:, cols].bitcast(FP8X4), scales=w1_scales[:, cols], in_=grouped[:])

        vw = [keep.tile([P, S], U32, name=f"vw{a}", align_bytes=64) for a in range(2)]
        vs = keep.tile([P, S], U8, name="vs", align_bytes=64)
        w4w = keep.tile([P, 2 * H], U8, name="w4w", align_bytes=64)
        w4s = keep.tile([P, H], U8, name="w4s", align_bytes=64)

        nc.vector.tensor_copy(
            out=w4w[:].bitcast(U16).rearrange("p (b t m) -> p b t m", b=NB, t=PACK),
            in_=w4w_raw[:].bitcast(U16).rearrange("p (b m t) -> p b t m", b=NB, t=PACK),
        )
        nc.vector.tensor_copy(
            out=w4s[:].rearrange("p (b t m) -> p b t m", b=NB, t=PACK),
            in_=w4s_raw[:].rearrange("p (b m t) -> p b t m", b=NB, t=PACK),
        )
        prepare_w1(0)
        nc.vector.tensor_copy(vw[0][:], tabw[0][:].indirect(offs_t[:]))
        nc.vector.tensor_copy(vs[:], tabs[:].indirect(offs_t[:]))
        bank_cuts = [slice(u * BANK, (u + 1) * BANK) for u in range(S // BANK)]
        for cols in bank_cuts:
            nc.vector.tensor_copy(vw[1][:, cols], tabw[1][:].indirect(offs_t[:, cols.start // 16 : cols.stop // 16]))

        th = {}
        banks = [f"bank{n}" for n in range(8)]

        def w1_pass(i, cols, bank):
            y = psum.tile([P, BANK], F32, name="y", tag=bank)
            ch = slice(i * P, (i + 1) * P)
            nc.tensor.matmul_mx(
                out=y[:, : cols.stop - cols.start],
                lhsT=w1_codes[:, ch].bitcast(FP8X4),
                lhsT_scale=w1_scales[:, ch],
                rhs=vw[0][:, cols].bitcast(FP8X4),
                rhs_scale=vs[4:P, cols],
                start=True,
                stop=False,
            )
            return y

        def w4_pass(i, cols, y):
            nc.tensor.matmul_mx(
                out=y[:, : cols.stop - cols.start],
                lhsT=w4w[:, 2 * i * P : 2 * (i + 1) * P].bitcast(FP4X4),
                lhsT_scale=w4s[:, i * P : (i + 1) * P],
                rhs=vw[1][:, cols].bitcast(FP8X4),
                rhs_scale=vs[:, cols],
                start=False,
                stop=True,
            )
            nc.scalar.activation(out=th[i][:, cols], in_=y[:, : cols.stop - cols.start], func=ACT.Tanh)

        def first_stage(i):
            th[i] = keep.tile([P, S], F32, name=f"th{i}", align_bytes=64)
            for u, cols in enumerate(bank_cuts):
                w4_pass(i, cols, w1_pass(i, cols, banks[(2 * i + u) % 4]))

        x2r = [keep.tile([P, PACK, M], BF16, name=f"x2r{b}", align_bytes=64) for b in range(NB)]
        n_tiles = NB * PACK

        def features(i, cols):
            b, t = divmod(i, PACK)
            nc.vector.scalar_tensor_tensor(
                out=th[i][:, cols],
                in0=th[i][:, cols],
                scalar=gain_t[:, b, t : t + 1],
                in1=law_t[i][:, cols],
                op0=MULT,
                op1=ADD,
            )

        def features_on_gpsimd(i, scaled):
            b, t = divmod(i, PACK)
            nc.gpsimd.tensor_scalar(
                out=scaled, in0=th[i][:], scalar1=gain_t[:, b, t : t + 1], scalar2=0.0, op0=MULT, op1=ADD
            )
            nc.gpsimd.tensor_tensor(out=th[i][:], in0=scaled, in1=law_t[i][:], op=ADD)

        def pick2(i, a2):
            b, t = divmod(i, PACK)
            g2 = keep.tile([P, M], F32, name=f"g2_{i}")
            nc.vector.tensor_copy(g2[:], th[i][:].indirect(pos2_t[:]))
            nc.scalar.activation(out=a2, in_=g2[:], func=ACT.Abs)
            nc.scalar.activation(out=x2r[b][:, t, :], in_=a2, func=ACT.Copy, scale=gv_t[:, b, t : t + 1])

        def pick1(i):
            nc.vector.tensor_copy(x1r[i // PACK][:, i % PACK, :], th[i][:].indirect(pos1_t[:]))


        def weave_and_quantise(src, cols, woven, name):
            width = cols.stop - cols.start
            nc.scalar.copy(
                out=woven.rearrange("p (c i t) -> p c t i", i=4, t=PACK),
                in_=src[:, :, cols].rearrange("p t (c i) -> p c t i", i=4),
            )
            codes = keep.tile([P, width], U32, name=name + "_codes", align_bytes=64)
            scales = keep.tile([P, width], U8, name=name + "_scales", align_bytes=64)
            nc.vector.quantize_mx(out=codes[:].bitcast(FP8X4), scales=scales[:], in_=woven)
            return codes, scales

        def score(c, b, c1, s1, c2, s2):
            nc.tensor.matmul_mx(
                out=e[c][:],
                lhsT=c1.bitcast(FP8X4),
                lhsT_scale=s1,
                rhs=c2[:].bitcast(FP8X4),
                rhs_scale=s2[:],
                start=(b == 0),
                stop=(b == NB - 1),
            )

        th[0] = keep.tile([P, S], F32, name="th0", align_bytes=64)
        opened = [w1_pass(0, cols, banks[u]) for u, cols in enumerate(bank_cuts)]
        for cols, y in zip(bank_cuts, opened):
            w4_pass(0, cols, y)
        first_stage(1)
        prepare_w1(1)
        for i in range(2, n_tiles):
            first_stage(i)
        e = [psum.tile([P, M], F32, name="e", tag=banks[4 + c]) for c in range(M // P)]
        x2q = {}
        x1r = {}

        def finish_x2(b):
            woven = keep.tile([P, M * PACK], BF16, name=f"x2_woven{b}", align_bytes=64)
            x2q[b] = weave_and_quantise(x2r[b][:], slice(0, M), woven[:], f"x2_{b}")

        for cols in bank_cuts:
            features(0, cols)
        early = n_tiles - 2
        for i in range(early):
            if i + 1 < early:
                features(i + 1, slice(0, S))
            a2 = keep.tile([P, M], F32, name=f"a2_{i % 2}", align_bytes=64)
            pick2(i, a2[:])
            if i == PACK - 1:
                finish_x2(0)
        first = keep.tile([P, PACK * M + S], F32, name="first", tag=f"law{early - 1}", align_bytes=64)
        x1r[0] = first[:, : PACK * M].rearrange("p (t m) -> p t m", t=PACK)
        for i in range(early, n_tiles):
            features_on_gpsimd(i, first[:, PACK * M :])
        for t in range(PACK):
            pick1(t)
        shared = keep.tile([P, (PACK + 2) * M], F32, name="shared", tag=f"a2_{(early - 1) % 2}", align_bytes=64)
        c1, s1 = weave_and_quantise(
            x1r[0], slice(0, M), shared[:, (PACK - 1) * M : (PACK + 1) * M].bitcast(BF16), "x1_0"
        )
        for i in range(early, n_tiles):
            pick2(i, shared[:, (PACK + 1) * M :])
        for c in range(M // P):
            score(c, 0, c1[:, c * P : (c + 1) * P], s1[:, c * P : (c + 1) * P], *x2q[0])
        x1r[1] = shared[:, : PACK * M].rearrange("p (t m) -> p t m", t=PACK)
        for t in range(PACK):
            pick1(PACK + t)
        finish_x2(1)
        woven = keep.tile([P, M * PACK], BF16, name="x1_woven1", tag=f"x2r{NB - 1}", align_bytes=64)
        for half in range(2):
            cols = slice(half * M // 2, (half + 1) * M // 2)
            c1, s1 = weave_and_quantise(
                x1r[1], cols, woven[:, cols.start * PACK : cols.stop * PACK], f"x1_1_{half}"
            )
            for c in range(2):
                score(2 * half + c, 1, c1[:, c * P : (c + 1) * P], s1[:, c * P : (c + 1) * P], *x2q[1])

        res = keep.tile([P, M // P, M], F32, name="res", tag=f"x2r{NB - 1}", align_bytes=64)
        for c in range(M // P):
            nc.vector.scalar_tensor_tensor(
                out=res[:, c, :], in0=e[c][:], scalar=colv_t[:, c : c + 1], in1=rowv_t[:], op0=MULT, op1=MULT
            )
            nc.sync.dma_start(out=out[c * P : (c + 1) * P, :], in_=res[:, c, :])
